import numpy as np
import ml_dtypes


def mxq(x, axis, fmt="e4m3"):
    dtype, down = {"e4m3": (ml_dtypes.float8_e4m3fn, 7), "e5m2": (ml_dtypes.float8_e5m2, 14)}[fmt]
    v = np.moveaxis(np.asarray(x, np.float32).astype(ml_dtypes.bfloat16).astype(np.float64), axis, -1)
    blocks = v.reshape(v.shape[:-1] + (-1, 32))
    amax = np.abs(blocks).max(-1, keepdims=True)
    byte = np.maximum(np.where(amax > 0, np.frexp(amax)[1] - 1 + 127, 0) - down, 1)
    scale = np.exp2(byte - 127.0)
    codes = (blocks / scale).astype(np.float32).astype(dtype).astype(np.float64)
    return np.moveaxis((codes * scale).reshape(v.shape), -1, axis)


WIDE = False


def mx_kscale(k):
    if not WIDE:
        return np.ones(k)
    levels = np.array([10, -10, 5, -5, 0])
    if k % 512:
        return np.exp2(np.random.permutation(np.resize(levels, k // 32))).repeat(32)
    a = np.empty((k // 512, 16))
    for p in range(k // 512):
        a[p, :8] = np.random.permutation(np.resize(levels, 8))
        for g in range(8):
            far = levels[np.abs(levels - a[p, g]) >= 10]
            a[p, g + 8] = far[np.random.randint(len(far))]
    return np.exp2(a.ravel()).repeat(32)


def f64(x):
    return np.asarray(x).astype(np.float64)


def striped8(idx):
    return np.asarray(idx).reshape(8, -1, 16).transpose(0, 2, 1).reshape(128, -1).astype(np.uint16)


def unstriped8(offs):
    return offs.reshape(8, 16, -1).transpose(0, 2, 1).reshape(8, -1).astype(np.int64)


def pick8(x, idx, run):
    r = np.arange(len(x))
    return x[r[:, None], idx[r % (8 * run) // run]]


E2M1 = np.array([0.0, 0.5, 1.0, 1.5, 2.0, 3.0, 4.0, 6.0, -0.0, -0.5, -1.0, -1.5, -2.0, -3.0, -4.0, -6.0])


def pack_weight(w, fmt):
    k, n = w.shape
    w = f64(np.asarray(w, np.float32).astype(ml_dtypes.bfloat16)).reshape(k // 32, 32, n)
    amax = np.abs(w).max(1)
    if fmt == "e4m3":
        byte = np.frexp(amax)[1] - 1 + 127 - 7
    else:
        mant, ex = np.frexp(amax / 6.0)
        byte = np.where(mant > 0.5, ex, ex - 1) + 127
    byte = np.clip(np.where(amax > 0, byte, 1), 1, 254)
    scaled = (w * np.exp2(127.0 - byte)[:, None, :]).reshape(k, n).astype(np.float32)
    by_word = np.ascontiguousarray(scaled.reshape(k // 512, 128, 4, n).transpose(0, 1, 3, 2))
    if fmt == "e4m3":
        words = by_word.astype(ml_dtypes.float8_e4m3fn).view(np.uint8)
    else:
        c = by_word.astype(ml_dtypes.float4_e2m1fn).view(np.uint8) & 0xF
        words = (c[..., 0::2] | (c[..., 1::2] << 4)).reshape(k // 512, 128, 2 * n)
    return np.ascontiguousarray(words), np.ascontiguousarray(byte.astype(np.uint8).reshape(k // 512, 16, n))


def unpack_weight(words, scales, fmt):
    g, _, n = scales.shape
    words = np.ascontiguousarray(words).reshape(g, 128, n, -1)
    if fmt == "e4m3":
        vals = words.view(ml_dtypes.float8_e4m3fn).astype(np.float64)
    else:
        nib = np.empty((g, 128, n, 4), np.uint8)
        nib[..., 0::2] = words & 0xF
        nib[..., 1::2] = words >> 4
        vals = E2M1[nib]
    vals = vals * np.repeat(np.exp2(scales.astype(np.float64) - 127.0), 8, axis=1)[..., None]
    return vals.transpose(0, 1, 3, 2).reshape(g * 512, n)


D, T, U, X, I, Q = 512, 1024, 1024, 1024, 512, 128


def setup_inputs():
    n = np.random.standard_normal
    idx = np.stack([np.random.permutation(T)[:I] for _ in range(8)])
    idx2 = np.stack([np.random.permutation(U)[:I] for _ in range(8)])
    idx3 = np.stack([np.random.permutation(X)[:I] for _ in range(8)])
    idx4 = np.stack([np.random.permutation(U)[:I] for _ in range(8)])
    idx5 = np.stack([np.random.permutation(U)[:I] for _ in range(8)])
    fd = mx_kscale(D)
    keysp = pack_weight(n((D, T)) / fd[:, None], "e4m3")
    notesp = pack_weight(n((D, U)) / fd[:, None], "e2m1")
    usersp = pack_weight(n((D, X)) / fd[:, None], "e4m3")
    return {
        "query": (n((D, Q)) * 1.0 / np.sqrt(D) * fd[:, None]).astype(np.float32),
        "keys_words": keysp[0],
        "keys_scales": keysp[1],
        "notes_words": notesp[0],
        "notes_scales": notesp[1],
        "users_words": usersp[0],
        "users_scales": usersp[1],
        "offs": striped8(idx),
        "offs2": striped8(idx2),
        "offs3": striped8(idx3),
        "offs4": striped8(idx4),
        "offs5": striped8(idx5),
    }


def reference(query, keys_words, keys_scales, notes_words, notes_scales, users_words, users_scales, offs, offs2, offs3, offs4, offs5):
    idx = unstriped8(offs)
    idx2 = unstriped8(offs2)
    idx3 = unstriped8(offs3)
    idx4 = unstriped8(offs4)
    idx5 = unstriped8(offs5)
    keysu = unpack_weight(keys_words, keys_scales, "e4m3")
    notesu = unpack_weight(notes_words, notes_scales, "e2m1")
    usersu = unpack_weight(users_words, users_scales, "e4m3")
    queryq = mxq(f64(query), 0, "e4m3")
    a = queryq.T @ keysu
    b = queryq.T @ notesu
    c0 = queryq.T @ usersu
    w = np.maximum(pick8(a, idx, 16), pick8(c0, idx3, 16))
    v = np.maximum(pick8(b, idx2, 16), pick8(c0, idx3, 16))
    r = w - v
    f1 = np.zeros((Q, U))
    f1[np.arange(Q)[:, None], idx4[np.arange(Q) % 128 // 16]] = r
    bb = b + f1
    y = pick8(bb, idx5, 16) + w
    return y

from contextlib import ExitStack

import concourse.mybir as mybir

D, POOL, SLOTS, Q = 512, 1024, 512, 128
FLOPS = 3 * 2 * D * Q * POOL

F32 = mybir.dt.float32
BF16 = mybir.dt.bfloat16
I32 = mybir.dt.int32
U32 = mybir.dt.uint32
U16 = mybir.dt.uint16
U8 = mybir.dt.uint8
FP8X4 = mybir.dt.float8_e4m3fn_x4
FP4X4 = mybir.dt.float4_e2m1fn_x4
ALU = mybir.AluOpType
COPY = mybir.ActivationFunctionType.Copy

P = 128
PACK = 4
HALF = SLOTS // 2
HALF_COLS = HALF // 16


def tile_attend_sharedrival_three_kernel(
    tc, query, keys_words, keys_scales, notes_words, notes_scales, users_words, users_scales,
    offs, offs2, offs3, offs4, offs5, out,
):
    nc = tc.nc

    with ExitStack() as ctx:
        keep = ctx.enter_context(tc.tile_pool(name="keep", bufs=1))
        psum = ctx.enter_context(tc.psum_pool(name="psum", bufs=1))

        token_list = keep.tile([P, SLOTS // 16], U16)
        note_list = keep.tile([P, SLOTS // 16], U16)
        user_list = keep.tile([P, SLOTS // 16], U16)
        put_list = keep.tile([P, SLOTS // 16], U16)
        read_list = keep.tile([P, SLOTS // 16], U16)

        q_raw = keep.tile([P, PACK, Q], F32)
        q_grouped = keep.tile([P, Q, PACK], BF16, align_bytes=64)
        q_codes = keep.tile([P, Q], U32, align_bytes=64)
        q_scales = keep.tile([P, Q], U8, align_bytes=64)
        users_codes = keep.tile([P, POOL], U32, align_bytes=64)
        keys_codes = keep.tile([P, POOL], U32, align_bytes=64)
        notes_codes = keep.tile([P, 2 * POOL], U8, align_bytes=64)
        users_plane = keep.tile([P, POOL], U8, align_bytes=64)
        keys_plane = keep.tile([P, POOL], U8, align_bytes=64)
        notes_plane = keep.tile([P, POOL], U8, align_bytes=64)

        a = keep.tile([P, POOL], F32)
        b = keep.tile([P, POOL], F32)
        c0 = keep.tile([P, POOL], F32)
        f1 = keep.tile([P, POOL], F32)
        bb = keep.tile([P, POOL], F32)
        token = keep.tile([P, SLOTS], F32)
        minus_note = keep.tile([P, SLOTS], F32)
        user = keep.tile([P, SLOTS], F32)
        w = keep.tile([P, SLOTS], F32)
        minus_v = keep.tile([P, SLOTS], F32)
        bb_late = keep.tile([P, HALF], F32)
        y = keep.tile([P, SLOTS], F32)

        def load_scales(queue, plane, scales):
            for quadrant in range(4):
                queue.dma_start(
                    plane[32 * quadrant : 32 * quadrant + 4, :].bitcast(I32),
                    scales[0, 4 * quadrant : 4 * quadrant + 4, :].bitcast(I32),
                )

        nc.vector.memset(users_plane[:].bitcast(I32), 0)
        nc.vector.memset(notes_plane[:].bitcast(I32), 0)
        nc.vector.memset(keys_plane[:].bitcast(I32), 0)
        nc.vector.memset(f1[:], 0.0)

        nc.sync.dma_start(q_raw[:], query.rearrange("(p t) q -> p t q", t=PACK))
        load_scales(nc.sync, users_plane, users_scales)
        nc.sync.dma_start(users_codes[:].bitcast(I32), users_words[0].rearrange("p n t -> p (n t)").bitcast(I32))
        load_scales(nc.sync, notes_plane, notes_scales)
        nc.sync.dma_start(user_list[:], offs3)
        nc.sync.dma_start(notes_codes[:].bitcast(I32), notes_words[0].bitcast(I32))
        nc.sync.dma_start(keys_codes[:].bitcast(I32), keys_words[0].rearrange("p n t -> p (n t)").bitcast(I32))
        load_scales(nc.sync, keys_plane, keys_scales)
        nc.sync.dma_start(note_list[:], offs2)
        nc.sync.dma_start(token_list[:], offs)
        nc.sync.dma_start(put_list[:], offs4)
        nc.sync.dma_start(read_list[:], offs5)

        nc.vector.tensor_copy(q_grouped[:], q_raw[:].rearrange("p t q -> p q t"))
        nc.vector.quantize_mx(
            out=q_codes[:].bitcast(FP8X4), scales=q_scales[:], in_=q_grouped[:].rearrange("p q t -> p (q t)")
        )

        def score(name, scores, first, last, codes, plane, on_vector):
            bank = psum.tile([Q, last - first], F32, name=name)
            nc.tensor.matmul_mx(
                out=bank[:], lhsT=q_codes[:].bitcast(FP8X4), lhsT_scale=q_scales[:],
                rhs=codes, rhs_scale=plane[:, first:last], start=True, stop=True,
            )
            if on_vector:
                nc.vector.tensor_copy(scores[:, first:last], bank[:])
            else:
                nc.scalar.activation(scores[:, first:last], bank[:], COPY)

        for first, last, on_vector in ((0, 512, False), (512, 768, True), (768, 1024, False)):
            score("users%d" % first, c0, first, last, users_codes[:, first:last].bitcast(FP8X4), users_plane, on_vector)
        for first, last in ((0, 512), (512, 1024)):
            score("notes%d" % first, b, first, last, notes_codes[:, 2 * first : 2 * last].bitcast(FP4X4), notes_plane, False)
        for first, last in ((0, 512), (512, 768), (768, 1024)):
            score("keys%d" % first, a, first, last, keys_codes[:, first:last].bitcast(FP8X4), keys_plane, False)

        early, late = slice(0, HALF), slice(HALF, SLOTS)
        early_cols, late_cols = slice(0, HALF_COLS), slice(HALF_COLS, 2 * HALF_COLS)

        nc.vector.tensor_copy(user[:], c0[:].indirect(user_list[:]))
        nc.vector.tensor_scalar(minus_note[:, early], b[:].indirect(note_list[:, early_cols]), -1.0, 0.0, ALU.mult, ALU.add)
        nc.vector.tensor_copy(token[:, early], a[:].indirect(token_list[:, early_cols]))
        nc.scalar.activation(minus_note[:, late], b[:].indirect(note_list[:, late_cols]), COPY, scale=-1.0)
        nc.scalar.activation(token[:, late], a[:].indirect(token_list[:, late_cols]), COPY)

        for slots, cols in ((early, early_cols), (late, late_cols)):
            nc.vector.scalar_tensor_tensor(minus_v[:, slots], user[:, slots], -1.0, minus_note[:, slots], ALU.mult, ALU.min)
            nc.vector.tensor_tensor(w[:, slots], token[:, slots], user[:, slots], ALU.max)
            nc.vector.tensor_tensor(f1[:].indirect(put_list[:, cols]), w[:, slots], minus_v[:, slots], ALU.add)

        nc.vector.tensor_tensor(bb[:], b[:], f1[:], ALU.add)

        nc.scalar.activation(bb_late[:], bb[:].indirect(read_list[:, late_cols]), COPY)
        nc.vector.tensor_tensor(y[:, early], bb[:].indirect(read_list[:, early_cols]), w[:, early], ALU.add)
        nc.sync.dma_start(out[:, early], y[:, early])
        nc.vector.tensor_tensor(y[:, late], bb_late[:], w[:, late], ALU.add)
        nc.scalar.dma_start(out[:, late], y[:, late])
